import numpy as np
import ml_dtypes


def mxq(x, axis, fmt="e4m3"):
    dtype, down = {"e4m3": (ml_dtypes.float8_e4m3fn, 7), "e5m2": (ml_dtypes.float8_e5m2, 14)}[fmt]
    v = np.moveaxis(np.asarray(x, np.float32).astype(ml_dtypes.bfloat16).astype(np.float64), axis, -1)
    blocks = v.reshape(v.shape[:-1] + (-1, 32))
    amax = np.abs(blocks).max(-1, keepdims=True)
    byte = np.maximum(np.where(amax > 0, np.frexp(amax)[1] - 1 + 127, 0) - down, 1)
    scale = np.exp2(byte - 127.0)
    codes = (blocks / scale).astype(np.float32).astype(dtype).astype(np.float64)
    return np.moveaxis((codes * scale).reshape(v.shape), -1, axis)


WIDE = False


def mx_kscale(k):
    if not WIDE:
        return np.ones(k)
    levels = np.array([10, -10, 5, -5, 0])
    if k % 512:
        return np.exp2(np.random.permutation(np.resize(levels, k // 32))).repeat(32)
    a = np.empty((k // 512, 16))
    for p in range(k // 512):
        a[p, :8] = np.random.permutation(np.resize(levels, 8))
        for g in range(8):
            far = levels[np.abs(levels - a[p, g]) >= 10]
            a[p, g + 8] = far[np.random.randint(len(far))]
    return np.exp2(a.ravel()).repeat(32)


def f64(x):
    return np.asarray(x).astype(np.float64)


def striped8(idx):
    return np.concatenate([v.reshape(-1, 16).T for v in idx]).astype(np.uint16)


def unstriped8(offs):
    return np.stack([offs[16 * g:16 * g + 16].T.reshape(-1) for g in range(8)]).astype(np.int64)


E2M1 = np.array([0.0, 0.5, 1.0, 1.5, 2.0, 3.0, 4.0, 6.0, -0.0, -0.5, -1.0, -1.5, -2.0, -3.0, -4.0, -6.0])


def pack_weight(w, fmt):
    k, n = w.shape
    w = f64(np.asarray(w, np.float32).astype(ml_dtypes.bfloat16)).reshape(k // 32, 32, n)
    amax = np.abs(w).max(1)
    if fmt == "e4m3":
        byte = np.frexp(amax)[1] - 1 + 127 - 7
    else:
        mant, ex = np.frexp(amax / 6.0)
        byte = np.where(mant > 0.5, ex, ex - 1) + 127
    byte = np.clip(np.where(amax > 0, byte, 1), 1, 254)
    scaled = (w * np.exp2(127.0 - byte)[:, None, :]).reshape(k, n).astype(np.float32)
    by_word = np.ascontiguousarray(scaled.reshape(k // 512, 128, 4, n).transpose(0, 1, 3, 2))
    if fmt == "e4m3":
        words = by_word.astype(ml_dtypes.float8_e4m3fn).view(np.uint8)
    else:
        c = by_word.astype(ml_dtypes.float4_e2m1fn).view(np.uint8) & 0xF
        words = (c[..., 0::2] | (c[..., 1::2] << 4)).reshape(k // 512, 128, 2 * n)
    return np.ascontiguousarray(words), np.ascontiguousarray(byte.astype(np.uint8).reshape(k // 512, 16, n))


def unpack_weight(words, scales, fmt):
    g, _, n = scales.shape
    words = np.ascontiguousarray(words).reshape(g, 128, n, -1)
    if fmt == "e4m3":
        vals = words.view(ml_dtypes.float8_e4m3fn).astype(np.float64)
    else:
        nib = np.empty((g, 128, n, 4), np.uint8)
        nib[..., 0::2] = words & 0xF
        nib[..., 1::2] = words >> 4
        vals = E2M1[nib]
    vals = vals * np.repeat(np.exp2(scales.astype(np.float64) - 127.0), 8, axis=1)[..., None]
    return vals.transpose(0, 1, 3, 2).reshape(g * 512, n)


K, M, T, S = 1536, 512, 512, 256


def setup_inputs():
    n = np.random.standard_normal
    s = mx_kscale(K)[:, None]
    p_w = pack_weight(n((K, M)) / np.sqrt(K) / s, "e2m1")
    return {
        "x": (n((K, S)) * s).astype(np.float32),
        "w_words": p_w[0],
        "w_scales": p_w[1],
        "b": (0.3 * n(512)).astype(np.float32),
        "wgo": np.repeat(np.random.uniform(0.5, 2.0, (8, S)), 16, axis=0).astype(np.float32),
        "offs": striped8(np.stack([np.random.permutation(T)[:S] for _ in range(8)])),
    }


def reference(x, w_words, w_scales, b, wgo, offs):
    x_ = mxq(f64(x), 0, "e4m3")
    w_ = unpack_weight(w_words, w_scales, "e2m1")
    y = w_.T @ x_
    place = unstriped8(offs)[np.arange(M) % 128 // 16]
    out = np.zeros((M, T))
    out[np.arange(M)[:, None], place] = f64(wgo)[np.arange(M) % 128] * (y + f64(b)[:, None])
    return out

@@ -1,0 +1,117 @@
+from contextlib import ExitStack
+
+import concourse.mybir as mybir
+
+F32 = mybir.dt.float32
+BF16 = mybir.dt.bfloat16
+I32 = mybir.dt.int32
+U32 = mybir.dt.uint32
+U16 = mybir.dt.uint16
+U8 = mybir.dt.uint8
+E4M3X4 = mybir.dt.float8_e4m3fn_x4
+E2M1X4 = mybir.dt.float4_e2m1fn_x4
+IDENTITY = mybir.ActivationFunctionType.Identity
+MULT = mybir.AluOpType.mult
+
+K, M, T, S = 1536, 512, 512, 256
+P = 128
+PACK = 4
+PASSES = K // (P * PACK)
+BLOCKS = M // P
+HALF = S // 2
+FLOPS = 2 * K * M * S
+
+
+def tile_list_hscat_bias_kernel(tc, x, w_words, w_scales, b, wgo, offs, out):
+    nc = tc.nc
+    with ExitStack() as ctx:
+        keep = ctx.enter_context(tc.tile_pool(name="keep", bufs=1))
+        psum = ctx.enter_context(tc.psum_pool(name="psum", bufs=1))
+
+        offs_t = keep.tile([P, S // 16], U16, name="offs_t")
+        w_t = keep.tile([P, PASSES, 2 * M], U8, name="w_t", align_bytes=64)
+        ws_t = keep.tile([P, PASSES, M], U8, name="ws_t", align_bytes=64)
+        wgo_t = keep.tile([P, S], F32, name="wgo_t")
+        b_rows = keep.tile([P, P], F32, name="b_rows", align_bytes=64)
+        b_cols = keep.tile([P, P], F32, name="b_cols", align_bytes=64)
+        warm_in = keep.tile([P, 1], F32, name="warm_in")
+        warm_out = keep.tile([P, 1], F32, name="warm_out")
+        windows = [keep.tile([P, T], F32, name=f"window{m}") for m in range(BLOCKS)]
+        raw_all = keep.tile([P, PASSES, PACK, S], F32, name="raw_all")
+        grouped = [[keep.tile([P, HALF, PACK], BF16, name=f"grouped{h}_{a}", align_bytes=64) for a in range(PASSES)] for h in range(2)]
+        codes = [[keep.tile([P, HALF], U32, name=f"codes{h}_{a}", align_bytes=64) for a in range(PASSES)] for h in range(2)]
+        scales = [[keep.tile([P, HALF], U8, name=f"scales{h}_{a}", align_bytes=64) for a in range(PASSES)] for h in range(2)]
+        biased = [[keep.tile([P, HALF], F32, name=f"biased{h}_{m}") for m in range(BLOCKS)] for h in range(2)]
+        sums = [[psum.tile([P, HALF], F32, name=f"sums{h}_{m}") for m in range(BLOCKS)] for h in range(2)]
+
+        def load_x(first, last):
+            rows = x[first * P * PACK : last * P * PACK, :].rearrange("(a p j) c -> p a (j c)", p=P, j=PACK)
+            nc.sync.dma_start(raw_all[:, first:last, :, :].rearrange("p a j c -> p a (j c)"), rows)
+
+        def load_w(lo, hi):
+            nc.sync.dma_start(w_t[:, :, 2 * lo : 2 * hi].bitcast(I32), w_words[:, :, 2 * lo : 2 * hi].bitcast(I32).rearrange("a p c -> p a c"))
+
+        def interleave(copy, a, lo, hi):
+            copy(out=grouped[lo // HALF][a][:, lo % HALF : lo % HALF + hi - lo, :], in_=raw_all[:, a, :, lo:hi].rearrange("p j c -> p c j"))
+
+        def quantize(h, a):
+            nc.vector.quantize_mx(
+                out=codes[h][a][:].bitcast(E4M3X4),
+                scales=scales[h][a][:],
+                in_=grouped[h][a][:].rearrange("p c j -> p (c j)"),
+            )
+
+        def multiply(h, a, m):
+            nc.tensor.matmul_mx(
+                out=sums[h][m][:],
+                lhsT=w_t[:, a, m * 2 * P : (m + 1) * 2 * P].bitcast(E2M1X4),
+                lhsT_scale=ws_t[:, a, m * P : (m + 1) * P],
+                rhs=codes[h][a][:].bitcast(E4M3X4),
+                rhs_scale=scales[h][a][:],
+                start=(a == 0),
+                stop=(a == PASSES - 1),
+            )
+
+        def add_bias(h, m):
+            nc.scalar.activation(biased[h][m][:], sums[h][m][:], IDENTITY, bias=b_cols[:, 32 * m : 32 * m + 1])
+
+        def scatter(h, m):
+            places = offs_t[:, h * HALF // 16 : (h + 1) * HALF // 16]
+            nc.vector.tensor_tensor(windows[m][:].indirect(places), biased[h][m][:], wgo_t[:, h * HALF : (h + 1) * HALF], MULT)
+
+        nc.gpsimd.memset(warm_in[:], 0.0)
+        nc.scalar.activation(warm_out[:], warm_in[:], IDENTITY)
+        nc.vector.memset(b_rows[:], 0.0)
+        ws_in = w_scales.bitcast(I32).rearrange("a (q r) n -> r q a n", r=4)
+        for r in range(4):
+            nc.scalar.dma_start(ws_t[r:P:32, :, :].bitcast(I32), ws_in[r])
+        load_x(0, 2)
+        nc.sync.dma_start(b_rows[0:P:32, :].rearrange("q (m i) -> q m i", m=BLOCKS), b.rearrange("(m q i) -> q m i", m=BLOCKS, q=4))
+        load_x(2, 3)
+        load_w(0, M // 2)
+        nc.sync.dma_start(offs_t[:], offs)
+        nc.sync.dma_start(wgo_t[:], wgo)
+        load_w(M // 2, M)
+        for m in range(BLOCKS):
+            nc.vector.memset(windows[m][:], 0.0)
+
+        for a in range(2):
+            interleave(nc.vector.tensor_copy, a, 0, HALF)
+            interleave(nc.scalar.copy, a, HALF, S)
+        for a in range(2):
+            quantize(0, a)
+        interleave(nc.vector.tensor_copy, 2, 0, HALF)
+        nc.vector.transpose(b_cols[:], b_rows[:])
+        quantize(0, 2)
+        interleave(nc.scalar.copy, 2, HALF, S)
+        for a in range(PASSES):
+            quantize(1, a)
+        for m0 in range(0, BLOCKS, 2):
+            for h in range(2):
+                for m in (m0, m0 + 1):
+                    for a in range(PASSES):
+                        multiply(h, a, m)
+                    add_bias(h, m)
+                    scatter(h, m)
+                    if h == 1:
+                        nc.sync.dma_start(out[m * P : (m + 1) * P, :], windows[m][:])

@@ -34,25 +34,29 @@ def tile_list_hscat_bias_kernel(tc, x, w_words, w_scales, b, wgo, offs, out):
         wgo_t = keep.tile([P, S], F32, name="wgo_t")
         b_rows = keep.tile([P, P], F32, name="b_rows", align_bytes=64)
         b_cols = keep.tile([P, P], F32, name="b_cols", align_bytes=64)
-        warm_in = keep.tile([P, 1], F32, name="warm_in")
-        warm_out = keep.tile([P, 1], F32, name="warm_out")
         windows = [keep.tile([P, T], F32, name=f"window{m}") for m in range(BLOCKS)]
-        raw_all = keep.tile([P, PASSES, PACK, S], F32, name="raw_all")
+        raw = [keep.tile([P, PACK, S], F32, name=f"raw{a}") for a in range(PASSES)]
         grouped = [[keep.tile([P, HALF, PACK], BF16, name=f"grouped{h}_{a}", align_bytes=64) for a in range(PASSES)] for h in range(2)]
         codes = [[keep.tile([P, HALF], U32, name=f"codes{h}_{a}", align_bytes=64) for a in range(PASSES)] for h in range(2)]
         scales = [[keep.tile([P, HALF], U8, name=f"scales{h}_{a}", align_bytes=64) for a in range(PASSES)] for h in range(2)]
-        biased = [[keep.tile([P, HALF], F32, name=f"biased{h}_{m}") for m in range(BLOCKS)] for h in range(2)]
+        biased = [keep.tile([P, S], F32, name=f"biased{m}") for m in range(BLOCKS)]
         sums = [[psum.tile([P, HALF], F32, name=f"sums{h}_{m}") for m in range(BLOCKS)] for h in range(2)]
 
-        def load_x(first, last):
-            rows = x[first * P * PACK : last * P * PACK, :].rearrange("(a p j) c -> p a (j c)", p=P, j=PACK)
-            nc.sync.dma_start(raw_all[:, first:last, :, :].rearrange("p a j c -> p a (j c)"), rows)
+        def load_x(a):
+            rows = x[a * P * PACK : (a + 1) * P * PACK, :].rearrange("(p j) c -> p (j c)", j=PACK)
+            nc.sync.dma_start(raw[a][:].rearrange("p j c -> p (j c)"), rows)
 
         def load_w(lo, hi):
             nc.sync.dma_start(w_t[:, :, 2 * lo : 2 * hi].bitcast(I32), w_words[:, :, 2 * lo : 2 * hi].bitcast(I32).rearrange("a p c -> p a c"))
 
-        def interleave(copy, a, lo, hi):
-            copy(out=grouped[lo // HALF][a][:, lo % HALF : lo % HALF + hi - lo, :], in_=raw_all[:, a, :, lo:hi].rearrange("p j c -> p c j"))
+        def on_scalar(out, in_):
+            nc.scalar.activation(out, in_, IDENTITY)
+
+        def interleave(copy, h, a, lo, hi):
+            copy(
+                out=grouped[h][a][:, lo:hi, :].rearrange("p (c i) j -> p c j i", i=4),
+                in_=raw[a][:, :, h * HALF + lo : h * HALF + hi].rearrange("p j (c i) -> p c j i", i=4),
+            )
 
         def quantize(h, a):
             nc.vector.quantize_mx(
@@ -61,57 +65,67 @@ def tile_list_hscat_bias_kernel(tc, x, w_words, w_scales, b, wgo, offs, out):
                 in_=grouped[h][a][:].rearrange("p c j -> p (c j)"),
             )
 
-        def multiply(h, a, m):
-            nc.tensor.matmul_mx(
-                out=sums[h][m][:],
-                lhsT=w_t[:, a, m * 2 * P : (m + 1) * 2 * P].bitcast(E2M1X4),
-                lhsT_scale=ws_t[:, a, m * P : (m + 1) * P],
-                rhs=codes[h][a][:].bitcast(E4M3X4),
-                rhs_scale=scales[h][a][:],
-                start=(a == 0),
-                stop=(a == PASSES - 1),
-            )
+        def multiply(h, m):
+            order = list(range(PASSES)) if (h, m) == (0, 0) else [PASSES - 1] + list(range(PASSES - 1))
+            for a in order:
+                nc.tensor.matmul_mx(
+                    out=sums[h][m][:],
+                    lhsT=w_t[:, a, m * 2 * P : (m + 1) * 2 * P].bitcast(E2M1X4),
+                    lhsT_scale=ws_t[:, a, m * P : (m + 1) * P],
+                    rhs=codes[h][a][:].bitcast(E4M3X4),
+                    rhs_scale=scales[h][a][:],
+                    start=(a == order[0]),
+                    stop=(a == order[-1]),
+                )
+            nc.scalar.activation(biased[m][:, h * HALF : (h + 1) * HALF], sums[h][m][:], IDENTITY, bias=b_cols[:, 32 * m : 32 * m + 1])
 
-        def add_bias(h, m):
-            nc.scalar.activation(biased[h][m][:], sums[h][m][:], IDENTITY, bias=b_cols[:, 32 * m : 32 * m + 1])
+        def scatter(m, lo, hi):
+            nc.vector.tensor_tensor(windows[m][:].indirect(offs_t[:, lo // 16 : hi // 16]), biased[m][:, lo:hi], wgo_t[:, lo:hi], MULT)
 
-        def scatter(h, m):
-            places = offs_t[:, h * HALF // 16 : (h + 1) * HALF // 16]
-            nc.vector.tensor_tensor(windows[m][:].indirect(places), biased[h][m][:], wgo_t[:, h * HALF : (h + 1) * HALF], MULT)
+        def store(m):
+            nc.sync.dma_start(out[m * P : (m + 1) * P, :], windows[m][:])
 
-        nc.gpsimd.memset(warm_in[:], 0.0)
-        nc.scalar.activation(warm_out[:], warm_in[:], IDENTITY)
-        nc.vector.memset(b_rows[:], 0.0)
+        nc.gpsimd.memset(b_rows[:], 0.0)
+        load_x(0)
+        nc.sync.dma_start(offs_t[:], offs)
+        nc.sync.dma_start(b_rows[0:P:32, :].rearrange("q (m i) -> q m i", m=BLOCKS), b.rearrange("(m q i) -> q m i", m=BLOCKS, q=4))
+        for a in range(1, PASSES):
+            load_x(a)
         ws_in = w_scales.bitcast(I32).rearrange("a (q r) n -> r q a n", r=4)
         for r in range(4):
-            nc.scalar.dma_start(ws_t[r:P:32, :, :].bitcast(I32), ws_in[r])
-        load_x(0, 2)
-        nc.sync.dma_start(b_rows[0:P:32, :].rearrange("q (m i) -> q m i", m=BLOCKS), b.rearrange("(m q i) -> q m i", m=BLOCKS, q=4))
-        load_x(2, 3)
+            nc.sync.dma_start(ws_t[r:P:32, :, :].bitcast(I32), ws_in[r])
         load_w(0, M // 2)
-        nc.sync.dma_start(offs_t[:], offs)
         nc.sync.dma_start(wgo_t[:], wgo)
         load_w(M // 2, M)
         for m in range(BLOCKS):
             nc.vector.memset(windows[m][:], 0.0)
-
-        for a in range(2):
-            interleave(nc.vector.tensor_copy, a, 0, HALF)
-            interleave(nc.scalar.copy, a, HALF, S)
-        for a in range(2):
-            quantize(0, a)
-        interleave(nc.vector.tensor_copy, 2, 0, HALF)
         nc.vector.transpose(b_cols[:], b_rows[:])
-        quantize(0, 2)
-        interleave(nc.scalar.copy, 2, HALF, S)
-        for a in range(PASSES):
+
+        for a in range(PASSES - 1):
+            interleave(nc.vector.tensor_copy, 0, a, 0, HALF)
+            interleave(nc.vector.tensor_copy, 1, a, 0, 32)
+            interleave(on_scalar, 1, a, 32, HALF)
+            quantize(0, a)
             quantize(1, a)
-        for m0 in range(0, BLOCKS, 2):
-            for h in range(2):
-                for m in (m0, m0 + 1):
-                    for a in range(PASSES):
-                        multiply(h, a, m)
-                    add_bias(h, m)
-                    scatter(h, m)
-                    if h == 1:
-                        nc.sync.dma_start(out[m * P : (m + 1) * P, :], windows[m][:])
+        a = PASSES - 1
+        interleave(nc.vector.tensor_copy, 0, a, 0, 80)
+        interleave(on_scalar, 0, a, 80, HALF)
+        interleave(nc.vector.tensor_copy, 1, a, 0, 64)
+        interleave(on_scalar, 1, a, 64, HALF)
+        quantize(0, a)
+        quantize(1, a)
+
+        multiply(0, 0)
+        scatter(0, 0, HALF)
+        multiply(0, 1)
+        multiply(1, 1)
+        scatter(1, 0, S)
+        store(1)
+        multiply(1, 0)
+        scatter(0, HALF, S)
+        store(0)
+        for m in range(2, BLOCKS):
+            multiply(0, m)
+            multiply(1, m)
+            scatter(m, 0, S)
+            store(m)

@@ -53,10 +53,7 @@ def tile_list_hscat_bias_kernel(tc, x, w_words, w_scales, b, wgo, offs, out):
             nc.scalar.activation(out, in_, IDENTITY)
 
         def interleave(copy, h, a, lo, hi):
-            copy(
-                out=grouped[h][a][:, lo:hi, :].rearrange("p (c i) j -> p c j i", i=4),
-                in_=raw[a][:, :, h * HALF + lo : h * HALF + hi].rearrange("p j (c i) -> p c j i", i=4),
-            )
+            copy(out=grouped[h][a][:, lo:hi, :], in_=raw[a][:, :, h * HALF + lo : h * HALF + hi].rearrange("p j c -> p c j"))
 
         def quantize(h, a):
             nc.vector.quantize_mx(
@@ -85,16 +82,16 @@ def tile_list_hscat_bias_kernel(tc, x, w_words, w_scales, b, wgo, offs, out):
         def store(m):
             nc.sync.dma_start(out[m * P : (m + 1) * P, :], windows[m][:])
 
-        nc.gpsimd.memset(b_rows[:], 0.0)
+        nc.vector.memset(b_rows[:], 0.0)
         load_x(0)
-        nc.sync.dma_start(offs_t[:], offs)
         nc.sync.dma_start(b_rows[0:P:32, :].rearrange("q (m i) -> q m i", m=BLOCKS), b.rearrange("(m q i) -> q m i", m=BLOCKS, q=4))
         for a in range(1, PASSES):
             load_x(a)
         ws_in = w_scales.bitcast(I32).rearrange("a (q r) n -> r q a n", r=4)
         for r in range(4):
-            nc.sync.dma_start(ws_t[r:P:32, :, :].bitcast(I32), ws_in[r])
+            nc.scalar.dma_start(ws_t[r:P:32, :, :].bitcast(I32), ws_in[r])
         load_w(0, M // 2)
+        nc.sync.dma_start(offs_t[:], offs)
         nc.sync.dma_start(wgo_t[:], wgo)
         load_w(M // 2, M)
         for m in range(BLOCKS):
@@ -115,15 +112,12 @@ def tile_list_hscat_bias_kernel(tc, x, w_words, w_scales, b, wgo, offs, out):
         quantize(0, a)
         quantize(1, a)
 
-        multiply(0, 0)
-        scatter(0, 0, HALF)
-        multiply(0, 1)
-        multiply(1, 1)
-        scatter(1, 0, S)
-        store(1)
-        multiply(1, 0)
-        scatter(0, HALF, S)
-        store(0)
+        for h in range(2):
+            for m in range(2):
+                multiply(h, m)
+                scatter(m, h * HALF, (h + 1) * HALF)
+                if h == 1:
+                    store(m)
         for m in range(2, BLOCKS):
             multiply(0, m)
             multiply(1, m)

@@ -29,25 +29,24 @@ def tile_list_hscat_bias_kernel(tc, x, w_words, w_scales, b, wgo, offs, out):
         psum = ctx.enter_context(tc.psum_pool(name="psum", bufs=1))
 
         offs_t = keep.tile([P, S // 16], U16, name="offs_t")
-        w_t = keep.tile([P, PASSES, 2 * M], U8, name="w_t", align_bytes=64)
+        w_first = keep.tile([P, PASSES, 2 * P], U8, name="w_first", align_bytes=64)
+        w_rest = keep.tile([P, PASSES, 2 * (M - P)], U8, name="w_rest", align_bytes=64)
         ws_t = keep.tile([P, PASSES, M], U8, name="ws_t", align_bytes=64)
         wgo_t = keep.tile([P, S], F32, name="wgo_t")
         b_rows = keep.tile([P, P], F32, name="b_rows", align_bytes=64)
-        b_cols = keep.tile([P, P], F32, name="b_cols", align_bytes=64)
         windows = [keep.tile([P, T], F32, name=f"window{m}") for m in range(BLOCKS)]
         raw = [keep.tile([P, PACK, S], F32, name=f"raw{a}") for a in range(PASSES)]
-        grouped = [[keep.tile([P, HALF, PACK], BF16, name=f"grouped{h}_{a}", align_bytes=64) for a in range(PASSES)] for h in range(2)]
+        grouped = [[keep.tile([P, HALF, PACK], BF16, name=f"grouped{h}_{a}", tag=f"grouped{h}_{a}", align_bytes=64) for a in range(PASSES)] for h in range(2)]
         codes = [[keep.tile([P, HALF], U32, name=f"codes{h}_{a}", align_bytes=64) for a in range(PASSES)] for h in range(2)]
         scales = [[keep.tile([P, HALF], U8, name=f"scales{h}_{a}", align_bytes=64) for a in range(PASSES)] for h in range(2)]
         biased = [keep.tile([P, S], F32, name=f"biased{m}") for m in range(BLOCKS)]
-        sums = [[psum.tile([P, HALF], F32, name=f"sums{h}_{m}") for m in range(BLOCKS)] for h in range(2)]
 
         def load_x(a):
             rows = x[a * P * PACK : (a + 1) * P * PACK, :].rearrange("(p j) c -> p (j c)", j=PACK)
             nc.sync.dma_start(raw[a][:].rearrange("p j c -> p (j c)"), rows)
 
-        def load_w(lo, hi):
-            nc.sync.dma_start(w_t[:, :, 2 * lo : 2 * hi].bitcast(I32), w_words[:, :, 2 * lo : 2 * hi].bitcast(I32).rearrange("a p c -> p a c"))
+        def load_w(tile, lo, hi):
+            nc.sync.dma_start(tile[:].bitcast(I32), w_words[:, :, 2 * lo : 2 * hi].bitcast(I32).rearrange("a p c -> p a c"))
 
         def on_scalar(out, in_):
             nc.scalar.activation(out, in_, IDENTITY)
@@ -62,19 +61,20 @@ def tile_list_hscat_bias_kernel(tc, x, w_words, w_scales, b, wgo, offs, out):
                 in_=grouped[h][a][:].rearrange("p c j -> p (c j)"),
             )
 
-        def multiply(h, m):
+        def multiply(h, m, bank):
+            sums = psum.tile([P, HALF], F32, name=f"sums{h}_{m}", tag=f"bank{bank}")
             order = list(range(PASSES)) if (h, m) == (0, 0) else [PASSES - 1] + list(range(PASSES - 1))
             for a in order:
                 nc.tensor.matmul_mx(
-                    out=sums[h][m][:],
-                    lhsT=w_t[:, a, m * 2 * P : (m + 1) * 2 * P].bitcast(E2M1X4),
+                    out=sums[:],
+                    lhsT=(w_first[:, a, :] if m == 0 else w_rest[:, a, (m - 1) * 2 * P : m * 2 * P]).bitcast(E2M1X4),
                     lhsT_scale=ws_t[:, a, m * P : (m + 1) * P],
                     rhs=codes[h][a][:].bitcast(E4M3X4),
                     rhs_scale=scales[h][a][:],
                     start=(a == order[0]),
                     stop=(a == order[-1]),
                 )
-            nc.scalar.activation(biased[m][:, h * HALF : (h + 1) * HALF], sums[h][m][:], IDENTITY, bias=b_cols[:, 32 * m : 32 * m + 1])
+            nc.scalar.activation(biased[m][:, h * HALF : (h + 1) * HALF], sums[:], IDENTITY, bias=b_cols[:, 32 * m : 32 * m + 1])
 
         def scatter(m, lo, hi):
             nc.vector.tensor_tensor(windows[m][:].indirect(offs_t[:, lo // 16 : hi // 16]), biased[m][:, lo:hi], wgo_t[:, lo:hi], MULT)
@@ -82,21 +82,19 @@ def tile_list_hscat_bias_kernel(tc, x, w_words, w_scales, b, wgo, offs, out):
         def store(m):
             nc.sync.dma_start(out[m * P : (m + 1) * P, :], windows[m][:])
 
-        nc.vector.memset(b_rows[:], 0.0)
-        load_x(0)
-        nc.sync.dma_start(b_rows[0:P:32, :].rearrange("q (m i) -> q m i", m=BLOCKS), b.rearrange("(m q i) -> q m i", m=BLOCKS, q=4))
-        for a in range(1, PASSES):
-            load_x(a)
+        nc.gpsimd.memset(b_rows[:], 0.0)
         ws_in = w_scales.bitcast(I32).rearrange("a (q r) n -> r q a n", r=4)
         for r in range(4):
             nc.scalar.dma_start(ws_t[r:P:32, :, :].bitcast(I32), ws_in[r])
-        load_w(0, M // 2)
         nc.sync.dma_start(offs_t[:], offs)
+        for a in range(PASSES):
+            load_x(a)
+        load_w(w_first, 0, P)
+        nc.sync.dma_start(b_rows[0:P:32, :].rearrange("q (m i) -> q m i", m=BLOCKS), b.rearrange("(m q i) -> q m i", m=BLOCKS, q=4))
         nc.sync.dma_start(wgo_t[:], wgo)
-        load_w(M // 2, M)
+        load_w(w_rest, P, M)
         for m in range(BLOCKS):
             nc.vector.memset(windows[m][:], 0.0)
-        nc.vector.transpose(b_cols[:], b_rows[:])
 
         for a in range(PASSES - 1):
             interleave(nc.vector.tensor_copy, 0, a, 0, HALF)
@@ -111,15 +109,24 @@ def tile_list_hscat_bias_kernel(tc, x, w_words, w_scales, b, wgo, offs, out):
         interleave(on_scalar, 1, a, 64, HALF)
         quantize(0, a)
         quantize(1, a)
+        b_cols = keep.tile([P, P], F32, name="b_cols", tag=f"grouped0_{a}", align_bytes=64)
+        nc.vector.transpose(b_cols[:], b_rows[:])
 
-        for h in range(2):
-            for m in range(2):
-                multiply(h, m)
-                scatter(m, h * HALF, (h + 1) * HALF)
-                if h == 1:
-                    store(m)
-        for m in range(2, BLOCKS):
-            multiply(0, m)
-            multiply(1, m)
-            scatter(m, 0, S)
-            store(m)
+        multiply(0, 0, 0)
+        scatter(0, 0, HALF)
+        multiply(0, 1, 1)
+        scatter(1, 0, HALF)
+        multiply(0, 2, 2)
+        multiply(1, 2, 3)
+        scatter(2, 0, S)
+        store(2)
+        multiply(1, 0, 1)
+        scatter(0, HALF, S)
+        store(0)
+        multiply(1, 1, 4)
+        scatter(1, HALF, S)
+        store(1)
+        multiply(0, 3, 5)
+        multiply(1, 3, 6)
+        scatter(3, 0, S)
+        store(3)

@@ -29,8 +29,8 @@ def tile_list_hscat_bias_kernel(tc, x, w_words, w_scales, b, wgo, offs, out):
         psum = ctx.enter_context(tc.psum_pool(name="psum", bufs=1))
 
         offs_t = keep.tile([P, S // 16], U16, name="offs_t")
-        w_first = keep.tile([P, PASSES, 2 * P], U8, name="w_first", align_bytes=64)
-        w_rest = keep.tile([P, PASSES, 2 * (M - P)], U8, name="w_rest", align_bytes=64)
+        w_first = keep.tile([P, PASSES, M], U8, name="w_first", align_bytes=64)
+        w_rest = keep.tile([P, PASSES, M], U8, name="w_rest", align_bytes=64)
         ws_t = keep.tile([P, PASSES, M], U8, name="ws_t", align_bytes=64)
         wgo_t = keep.tile([P, S], F32, name="wgo_t")
         b_rows = keep.tile([P, P], F32, name="b_rows", align_bytes=64)
@@ -67,7 +67,7 @@ def tile_list_hscat_bias_kernel(tc, x, w_words, w_scales, b, wgo, offs, out):
             for a in order:
                 nc.tensor.matmul_mx(
                     out=sums[:],
-                    lhsT=(w_first[:, a, :] if m == 0 else w_rest[:, a, (m - 1) * 2 * P : m * 2 * P]).bitcast(E2M1X4),
+                    lhsT=(w_first, w_rest)[m // 2][:, a, m % 2 * 2 * P : (m % 2 + 1) * 2 * P].bitcast(E2M1X4),
                     lhsT_scale=ws_t[:, a, m * P : (m + 1) * P],
                     rhs=codes[h][a][:].bitcast(E4M3X4),
                     rhs_scale=scales[h][a][:],
@@ -86,13 +86,13 @@ def tile_list_hscat_bias_kernel(tc, x, w_words, w_scales, b, wgo, offs, out):
         ws_in = w_scales.bitcast(I32).rearrange("a (q r) n -> r q a n", r=4)
         for r in range(4):
             nc.scalar.dma_start(ws_t[r:P:32, :, :].bitcast(I32), ws_in[r])
-        nc.sync.dma_start(offs_t[:], offs)
         for a in range(PASSES):
             load_x(a)
-        load_w(w_first, 0, P)
+        load_w(w_first, 0, M // 2)
         nc.sync.dma_start(b_rows[0:P:32, :].rearrange("q (m i) -> q m i", m=BLOCKS), b.rearrange("(m q i) -> q m i", m=BLOCKS, q=4))
+        nc.sync.dma_start(offs_t[:], offs)
         nc.sync.dma_start(wgo_t[:], wgo)
-        load_w(w_rest, P, M)
+        load_w(w_rest, M // 2, M)
         for m in range(BLOCKS):
             nc.vector.memset(windows[m][:], 0.0)
 
@@ -112,21 +112,14 @@ def tile_list_hscat_bias_kernel(tc, x, w_words, w_scales, b, wgo, offs, out):
         b_cols = keep.tile([P, P], F32, name="b_cols", tag=f"grouped0_{a}", align_bytes=64)
         nc.vector.transpose(b_cols[:], b_rows[:])
 
-        multiply(0, 0, 0)
-        scatter(0, 0, HALF)
-        multiply(0, 1, 1)
-        scatter(1, 0, HALF)
-        multiply(0, 2, 2)
-        multiply(1, 2, 3)
-        scatter(2, 0, S)
-        store(2)
-        multiply(1, 0, 1)
-        scatter(0, HALF, S)
-        store(0)
-        multiply(1, 1, 4)
-        scatter(1, HALF, S)
-        store(1)
-        multiply(0, 3, 5)
-        multiply(1, 3, 6)
-        scatter(3, 0, S)
-        store(3)
+        for h in range(2):
+            for m in range(2):
+                multiply(h, m, 2 * m + h)
+                scatter(m, h * HALF, (h + 1) * HALF)
+                if h == 1:
+                    store(m)
+        for m in range(2, BLOCKS):
+            for h in range(2):
+                multiply(h, m, 2 * m + h)
+            scatter(m, 0, S)
+            store(m)

@@ -33,7 +33,7 @@ def tile_list_hscat_bias_kernel(tc, x, w_words, w_scales, b, wgo, offs, out):
         w_rest = keep.tile([P, PASSES, M], U8, name="w_rest", align_bytes=64)
         ws_t = keep.tile([P, PASSES, M], U8, name="ws_t", align_bytes=64)
         wgo_t = keep.tile([P, S], F32, name="wgo_t")
-        b_rows = keep.tile([P, P], F32, name="b_rows", align_bytes=64)
+        b_cols = keep.tile([P, BLOCKS], F32, name="b_cols")
         windows = [keep.tile([P, T], F32, name=f"window{m}") for m in range(BLOCKS)]
         raw = [keep.tile([P, PACK, S], F32, name=f"raw{a}") for a in range(PASSES)]
         grouped = [[keep.tile([P, HALF, PACK], BF16, name=f"grouped{h}_{a}", tag=f"grouped{h}_{a}", align_bytes=64) for a in range(PASSES)] for h in range(2)]
@@ -52,7 +52,10 @@ def tile_list_hscat_bias_kernel(tc, x, w_words, w_scales, b, wgo, offs, out):
             nc.scalar.activation(out, in_, IDENTITY)
 
         def interleave(copy, h, a, lo, hi):
-            copy(out=grouped[h][a][:, lo:hi, :], in_=raw[a][:, :, h * HALF + lo : h * HALF + hi].rearrange("p j c -> p c j"))
+            copy(
+                out=grouped[h][a][:, lo:hi, :].rearrange("p (c i) j -> p c j i", i=4),
+                in_=raw[a][:, :, h * HALF + lo : h * HALF + hi].rearrange("p j (c i) -> p c j i", i=4),
+            )
 
         def quantize(h, a):
             nc.vector.quantize_mx(
@@ -74,7 +77,7 @@ def tile_list_hscat_bias_kernel(tc, x, w_words, w_scales, b, wgo, offs, out):
                     start=(a == order[0]),
                     stop=(a == order[-1]),
                 )
-            nc.scalar.activation(biased[m][:, h * HALF : (h + 1) * HALF], sums[:], IDENTITY, bias=b_cols[:, 32 * m : 32 * m + 1])
+            nc.scalar.activation(biased[m][:, h * HALF : (h + 1) * HALF], sums[:], IDENTITY, bias=b_cols[:, m : m + 1])
 
         def scatter(m, lo, hi):
             nc.vector.tensor_tensor(windows[m][:].indirect(offs_t[:, lo // 16 : hi // 16]), biased[m][:, lo:hi], wgo_t[:, lo:hi], MULT)
@@ -82,14 +85,14 @@ def tile_list_hscat_bias_kernel(tc, x, w_words, w_scales, b, wgo, offs, out):
         def store(m):
             nc.sync.dma_start(out[m * P : (m + 1) * P, :], windows[m][:])
 
-        nc.gpsimd.memset(b_rows[:], 0.0)
         ws_in = w_scales.bitcast(I32).rearrange("a (q r) n -> r q a n", r=4)
         for r in range(4):
             nc.scalar.dma_start(ws_t[r:P:32, :, :].bitcast(I32), ws_in[r])
         for a in range(PASSES):
             load_x(a)
         load_w(w_first, 0, M // 2)
-        nc.sync.dma_start(b_rows[0:P:32, :].rearrange("q (m i) -> q m i", m=BLOCKS), b.rearrange("(m q i) -> q m i", m=BLOCKS, q=4))
+        with nc.allow_non_contiguous_dma(reason="one bias value a partition and block"):
+            nc.sync.dma_start(b_cols[:], b.rearrange("(m p) -> p m", p=P))
         nc.sync.dma_start(offs_t[:], offs)
         nc.sync.dma_start(wgo_t[:], wgo)
         load_w(w_rest, M // 2, M)
@@ -109,8 +112,6 @@ def tile_list_hscat_bias_kernel(tc, x, w_words, w_scales, b, wgo, offs, out):
         interleave(on_scalar, 1, a, 64, HALF)
         quantize(0, a)
         quantize(1, a)
-        b_cols = keep.tile([P, P], F32, name="b_cols", tag=f"grouped0_{a}", align_bytes=64)
-        nc.vector.transpose(b_cols[:], b_rows[:])
 
         for h in range(2):
             for m in range(2):

@@ -29,9 +29,11 @@ def tile_list_hscat_bias_kernel(tc, x, w_words, w_scales, b, wgo, offs, out):
         psum = ctx.enter_context(tc.psum_pool(name="psum", bufs=1))
 
         offs_t = keep.tile([P, S // 16], U16, name="offs_t")
-        w_first = keep.tile([P, PASSES, M], U8, name="w_first", align_bytes=64)
+        w_early = keep.tile([P, PASSES - 1, M], U8, name="w_early", align_bytes=64)
+        w_last = keep.tile([P, 1, M], U8, name="w_last", align_bytes=64)
         w_rest = keep.tile([P, PASSES, M], U8, name="w_rest", align_bytes=64)
-        ws_t = keep.tile([P, PASSES, M], U8, name="ws_t", align_bytes=64)
+        ws_first = keep.tile([P, PASSES, M // 2], U8, name="ws_first", align_bytes=64)
+        ws_rest = keep.tile([P, PASSES, M // 2], U8, name="ws_rest", align_bytes=64)
         wgo_t = keep.tile([P, S], F32, name="wgo_t")
         b_cols = keep.tile([P, BLOCKS], F32, name="b_cols")
         windows = [keep.tile([P, T], F32, name=f"window{m}") for m in range(BLOCKS)]
@@ -45,8 +47,13 @@ def tile_list_hscat_bias_kernel(tc, x, w_words, w_scales, b, wgo, offs, out):
             rows = x[a * P * PACK : (a + 1) * P * PACK, :].rearrange("(p j) c -> p (j c)", j=PACK)
             nc.sync.dma_start(raw[a][:].rearrange("p j c -> p (j c)"), rows)
 
-        def load_w(tile, lo, hi):
-            nc.sync.dma_start(tile[:].bitcast(I32), w_words[:, :, 2 * lo : 2 * hi].bitcast(I32).rearrange("a p c -> p a c"))
+        def load_w(tile, first, last, lo, hi):
+            nc.sync.dma_start(tile[:].bitcast(I32), w_words[first:last, :, 2 * lo : 2 * hi].bitcast(I32).rearrange("a p c -> p a c"))
+
+        def load_scales(queue, tile, lo, hi):
+            rows = w_scales[:, :, lo:hi].bitcast(I32).rearrange("a (q r) n -> r q a n", r=4)
+            for r in range(4):
+                queue.dma_start(tile[r:P:32, :, :].bitcast(I32), rows[r])
 
         def on_scalar(out, in_):
             nc.scalar.activation(out, in_, IDENTITY)
@@ -64,14 +71,20 @@ def tile_list_hscat_bias_kernel(tc, x, w_words, w_scales, b, wgo, offs, out):
                 in_=grouped[h][a][:].rearrange("p c j -> p (c j)"),
             )
 
+        def weights(a, m):
+            cols = slice(m % 2 * 2 * P, (m % 2 + 1) * 2 * P)
+            if m >= 2:
+                return w_rest[:, a, cols]
+            return w_early[:, a, cols] if a < PASSES - 1 else w_last[:, 0, cols]
+
         def multiply(h, m, bank):
             sums = psum.tile([P, HALF], F32, name=f"sums{h}_{m}", tag=f"bank{bank}")
             order = list(range(PASSES)) if (h, m) == (0, 0) else [PASSES - 1] + list(range(PASSES - 1))
             for a in order:
                 nc.tensor.matmul_mx(
                     out=sums[:],
-                    lhsT=(w_first, w_rest)[m // 2][:, a, m % 2 * 2 * P : (m % 2 + 1) * 2 * P].bitcast(E2M1X4),
-                    lhsT_scale=ws_t[:, a, m * P : (m + 1) * P],
+                    lhsT=weights(a, m).bitcast(E2M1X4),
+                    lhsT_scale=(ws_first, ws_rest)[m // 2][:, a, m % 2 * P : (m % 2 + 1) * P],
                     rhs=codes[h][a][:].bitcast(E4M3X4),
                     rhs_scale=scales[h][a][:],
                     start=(a == order[0]),
@@ -83,19 +96,22 @@ def tile_list_hscat_bias_kernel(tc, x, w_words, w_scales, b, wgo, offs, out):
             nc.vector.tensor_tensor(windows[m][:].indirect(offs_t[:, lo // 16 : hi // 16]), biased[m][:, lo:hi], wgo_t[:, lo:hi], MULT)
 
         def store(m):
-            nc.sync.dma_start(out[m * P : (m + 1) * P, :], windows[m][:])
+            pieces = 1 if m == BLOCKS - 1 else 2
+            for lo in range(0, T, T // pieces):
+                nc.sync.dma_start(out[m * P : (m + 1) * P, lo : lo + T // pieces], windows[m][:, lo : lo + T // pieces])
 
-        ws_in = w_scales.bitcast(I32).rearrange("a (q r) n -> r q a n", r=4)
-        for r in range(4):
-            nc.scalar.dma_start(ws_t[r:P:32, :, :].bitcast(I32), ws_in[r])
-        for a in range(PASSES):
+        load_scales(nc.scalar, ws_first, 0, M // 2)
+        load_x(0)
+        nc.sync.dma_start(offs_t[:], offs)
+        for a in range(1, PASSES):
             load_x(a)
-        load_w(w_first, 0, M // 2)
+        load_w(w_early, 0, PASSES - 1, 0, M // 2)
+        load_w(w_last, PASSES - 1, PASSES, 0, M // 2)
         with nc.allow_non_contiguous_dma(reason="one bias value a partition and block"):
             nc.sync.dma_start(b_cols[:], b.rearrange("(m p) -> p m", p=P))
-        nc.sync.dma_start(offs_t[:], offs)
         nc.sync.dma_start(wgo_t[:], wgo)
-        load_w(w_rest, M // 2, M)
+        load_w(w_rest, 0, PASSES, M // 2, M)
+        load_scales(nc.sync, ws_rest, M // 2, M)
         for m in range(BLOCKS):
             nc.vector.memset(windows[m][:], 0.0)
 

@@ -35,7 +35,8 @@ def tile_list_hscat_bias_kernel(tc, x, w_words, w_scales, b, wgo, offs, out):
         ws_first = keep.tile([P, PASSES, M // 2], U8, name="ws_first", align_bytes=64)
         ws_rest = keep.tile([P, PASSES, M // 2], U8, name="ws_rest", align_bytes=64)
         wgo_t = keep.tile([P, S], F32, name="wgo_t")
-        b_cols = keep.tile([P, BLOCKS], F32, name="b_cols")
+        b_first = keep.tile([P, 2], F32, name="b_first")
+        b_rest = keep.tile([P, 2], F32, name="b_rest")
         windows = [keep.tile([P, T], F32, name=f"window{m}") for m in range(BLOCKS)]
         raw = [keep.tile([P, PACK, S], F32, name=f"raw{a}") for a in range(PASSES)]
         grouped = [[keep.tile([P, HALF, PACK], BF16, name=f"grouped{h}_{a}", tag=f"grouped{h}_{a}", align_bytes=64) for a in range(PASSES)] for h in range(2)]
@@ -54,6 +55,10 @@ def tile_list_hscat_bias_kernel(tc, x, w_words, w_scales, b, wgo, offs, out):
             rows = w_scales[:, :, lo:hi].bitcast(I32).rearrange("a (q r) n -> r q a n", r=4)
             for r in range(4):
                 queue.dma_start(tile[r:P:32, :, :].bitcast(I32), rows[r])
+
+        def load_bias(tile, first, last):
+            with nc.allow_non_contiguous_dma(reason="one bias value a partition and block"):
+                nc.sync.dma_start(tile[:], b.rearrange("(m p) -> p m", p=P)[:, first:last])
 
         def on_scalar(out, in_):
             nc.scalar.activation(out, in_, IDENTITY)
@@ -90,27 +95,27 @@ def tile_list_hscat_bias_kernel(tc, x, w_words, w_scales, b, wgo, offs, out):
                     start=(a == order[0]),
                     stop=(a == order[-1]),
                 )
-            nc.scalar.activation(biased[m][:, h * HALF : (h + 1) * HALF], sums[:], IDENTITY, bias=b_cols[:, m : m + 1])
+            nc.scalar.activation(biased[m][:, h * HALF : (h + 1) * HALF], sums[:], IDENTITY, bias=(b_first, b_rest)[m // 2][:, m % 2 : m % 2 + 1])
 
         def scatter(m, lo, hi):
             nc.vector.tensor_tensor(windows[m][:].indirect(offs_t[:, lo // 16 : hi // 16]), biased[m][:, lo:hi], wgo_t[:, lo:hi], MULT)
 
         def store(m):
-            pieces = 1 if m == BLOCKS - 1 else 2
+            pieces = 1 if m >= 2 else 2
             for lo in range(0, T, T // pieces):
                 nc.sync.dma_start(out[m * P : (m + 1) * P, lo : lo + T // pieces], windows[m][:, lo : lo + T // pieces])
 
-        load_scales(nc.scalar, ws_first, 0, M // 2)
         load_x(0)
-        nc.sync.dma_start(offs_t[:], offs)
+        load_scales(nc.sync, ws_first, 0, M // 2)
         for a in range(1, PASSES):
             load_x(a)
         load_w(w_early, 0, PASSES - 1, 0, M // 2)
         load_w(w_last, PASSES - 1, PASSES, 0, M // 2)
-        with nc.allow_non_contiguous_dma(reason="one bias value a partition and block"):
-            nc.sync.dma_start(b_cols[:], b.rearrange("(m p) -> p m", p=P))
+        load_bias(b_first, 0, 2)
+        nc.sync.dma_start(offs_t[:], offs)
         nc.sync.dma_start(wgo_t[:], wgo)
         load_w(w_rest, 0, PASSES, M // 2, M)
+        load_bias(b_rest, 2, BLOCKS)
         load_scales(nc.sync, ws_rest, M // 2, M)
         for m in range(BLOCKS):
             nc.vector.memset(windows[m][:], 0.0)

@@ -51,9 +51,9 @@ def tile_list_hscat_bias_kernel(tc, x, w_words, w_scales, b, wgo, offs, out):
         def load_w(tile, first, last, lo, hi):
             nc.sync.dma_start(tile[:].bitcast(I32), w_words[first:last, :, 2 * lo : 2 * hi].bitcast(I32).rearrange("a p c -> p a c"))
 
-        def load_scales(queue, tile, lo, hi):
+        def load_scales(queue, tile, lo, hi, first=0, end=4):
             rows = w_scales[:, :, lo:hi].bitcast(I32).rearrange("a (q r) n -> r q a n", r=4)
-            for r in range(4):
+            for r in range(first, end):
                 queue.dma_start(tile[r:P:32, :, :].bitcast(I32), rows[r])
 
         def load_bias(tile, first, last):
@@ -69,11 +69,11 @@ def tile_list_hscat_bias_kernel(tc, x, w_words, w_scales, b, wgo, offs, out):
                 in_=raw[a][:, :, h * HALF + lo : h * HALF + hi].rearrange("p j (c i) -> p c j i", i=4),
             )
 
-        def quantize(h, a):
+        def quantize(h, a, lo=0, hi=HALF):
             nc.vector.quantize_mx(
-                out=codes[h][a][:].bitcast(E4M3X4),
-                scales=scales[h][a][:],
-                in_=grouped[h][a][:].rearrange("p c j -> p (c j)"),
+                out=codes[h][a][:, lo:hi].bitcast(E4M3X4),
+                scales=scales[h][a][:, lo:hi],
+                in_=grouped[h][a][:, lo:hi, :].rearrange("p c j -> p (c j)"),
             )
 
         def weights(a, m):
@@ -106,9 +106,10 @@ def tile_list_hscat_bias_kernel(tc, x, w_words, w_scales, b, wgo, offs, out):
                 nc.sync.dma_start(out[m * P : (m + 1) * P, lo : lo + T // pieces], windows[m][:, lo : lo + T // pieces])
 
         load_x(0)
-        load_scales(nc.sync, ws_first, 0, M // 2)
+        load_scales(nc.sync, ws_first, 0, M // 2, 0, 2)
         for a in range(1, PASSES):
             load_x(a)
+        load_scales(nc.sync, ws_first, 0, M // 2, 2, 4)
         load_w(w_early, 0, PASSES - 1, 0, M // 2)
         load_w(w_last, PASSES - 1, PASSES, 0, M // 2)
         load_bias(b_first, 0, 2)
@@ -127,11 +128,13 @@ def tile_list_hscat_bias_kernel(tc, x, w_words, w_scales, b, wgo, offs, out):
             quantize(0, a)
             quantize(1, a)
         a = PASSES - 1
-        interleave(nc.vector.tensor_copy, 0, a, 0, 80)
-        interleave(on_scalar, 0, a, 80, HALF)
-        interleave(nc.vector.tensor_copy, 1, a, 0, 64)
-        interleave(on_scalar, 1, a, 64, HALF)
-        quantize(0, a)
+        interleave(nc.vector.tensor_copy, 0, a, 0, 64)
+        interleave(nc.vector.tensor_copy, 0, a, 64, 96)
+        interleave(on_scalar, 0, a, 96, HALF)
+        interleave(nc.vector.tensor_copy, 1, a, 0, 32)
+        interleave(on_scalar, 1, a, 32, HALF)
+        quantize(0, a, 0, 64)
+        quantize(0, a, 64, HALF)
         quantize(1, a)
 
         for h in range(2):

@@ -129,10 +129,8 @@ def tile_list_hscat_bias_kernel(tc, x, w_words, w_scales, b, wgo, offs, out):
             quantize(1, a)
         a = PASSES - 1
         interleave(nc.vector.tensor_copy, 0, a, 0, 64)
-        interleave(nc.vector.tensor_copy, 0, a, 64, 96)
-        interleave(on_scalar, 0, a, 96, HALF)
-        interleave(nc.vector.tensor_copy, 1, a, 0, 32)
-        interleave(on_scalar, 1, a, 32, HALF)
+        interleave(nc.vector.tensor_copy, 0, a, 64, HALF)
+        interleave(on_scalar, 1, a, 0, HALF)
         quantize(0, a, 0, 64)
         quantize(0, a, 64, HALF)
         quantize(1, a)

@@ -12,6 +12,7 @@ E4M3X4 = mybir.dt.float8_e4m3fn_x4
 E2M1X4 = mybir.dt.float4_e2m1fn_x4
 IDENTITY = mybir.ActivationFunctionType.Identity
 MULT = mybir.AluOpType.mult
+ADD = mybir.AluOpType.add
 
 K, M, T, S = 1536, 512, 512, 256
 P = 128
@@ -61,7 +62,7 @@ def tile_list_hscat_bias_kernel(tc, x, w_words, w_scales, b, wgo, offs, out):
                 nc.sync.dma_start(tile[:], b.rearrange("(m p) -> p m", p=P)[:, first:last])
 
         def on_scalar(out, in_):
-            nc.scalar.activation(out, in_, IDENTITY)
+            nc.scalar.copy(out, in_)
 
         def interleave(copy, h, a, lo, hi):
             copy(
@@ -95,7 +96,11 @@ def tile_list_hscat_bias_kernel(tc, x, w_words, w_scales, b, wgo, offs, out):
                     start=(a == order[0]),
                     stop=(a == order[-1]),
                 )
-            nc.scalar.activation(biased[m][:, h * HALF : (h + 1) * HALF], sums[:], IDENTITY, bias=(b_first, b_rest)[m // 2][:, m % 2 : m % 2 + 1])
+            bias = (b_first, b_rest)[m // 2][:, m % 2 : m % 2 + 1]
+            if (h, m) == (0, 0):
+                nc.vector.tensor_scalar(biased[m][:, :HALF], sums[:], bias, None, ADD)
+            else:
+                nc.scalar.activation(biased[m][:, h * HALF : (h + 1) * HALF], sums[:], IDENTITY, bias=bias)
 
         def scatter(m, lo, hi):
             nc.vector.tensor_tensor(windows[m][:].indirect(offs_t[:, lo // 16 : hi // 16]), biased[m][:, lo:hi], wgo_t[:, lo:hi], MULT)

@@ -18,8 +18,9 @@ K, M, T, S = 1536, 512, 512, 256
 P = 128
 PACK = 4
 PASSES = K // (P * PACK)
-BLOCKS = M // P
+BANDS = M // P
 HALF = S // 2
+PIECE = HALF // 2
 FLOPS = 2 * K * M * S
 
 
@@ -33,48 +34,48 @@ def tile_list_hscat_bias_kernel(tc, x, w_words, w_scales, b, wgo, offs, out):
         w_early = keep.tile([P, PASSES - 1, M], U8, name="w_early", align_bytes=64)
         w_last = keep.tile([P, 1, M], U8, name="w_last", align_bytes=64)
         w_rest = keep.tile([P, PASSES, M], U8, name="w_rest", align_bytes=64)
-        ws_first = keep.tile([P, PASSES, M // 2], U8, name="ws_first", align_bytes=64)
-        ws_rest = keep.tile([P, PASSES, M // 2], U8, name="ws_rest", align_bytes=64)
-        wgo_t = keep.tile([P, S], F32, name="wgo_t")
-        b_first = keep.tile([P, 2], F32, name="b_first")
-        b_rest = keep.tile([P, 2], F32, name="b_rest")
-        windows = [keep.tile([P, T], F32, name=f"window{m}") for m in range(BLOCKS)]
-        raw = [keep.tile([P, PACK, S], F32, name=f"raw{a}") for a in range(PASSES)]
-        grouped = [[keep.tile([P, HALF, PACK], BF16, name=f"grouped{h}_{a}", tag=f"grouped{h}_{a}", align_bytes=64) for a in range(PASSES)] for h in range(2)]
+        ws = keep.tile([P, 2 * PASSES + 1, M], U8, name="ws", align_bytes=64)
+        wgo_t = [keep.tile([P, HALF], F32, name=f"wgo{h}") for h in range(2)]
+        b_rows = keep.tile([BANDS, P], F32, name="b_rows")
+        b_blocks = keep.tile([P, 32], F32, name="b_blocks", align_bytes=64)
+        b_late = keep.tile([P, 32], F32, name="b_late", align_bytes=64)
+        windows = [keep.tile([P, T], F32, name=f"window{m}") for m in range(BANDS)]
         codes = [[keep.tile([P, HALF], U32, name=f"codes{h}_{a}", align_bytes=64) for a in range(PASSES)] for h in range(2)]
         scales = [[keep.tile([P, HALF], U8, name=f"scales{h}_{a}", align_bytes=64) for a in range(PASSES)] for h in range(2)]
-        biased = [keep.tile([P, S], F32, name=f"biased{m}") for m in range(BLOCKS)]
+        x_rows = x.rearrange("(a p j) c -> a p j c", p=P, j=PACK)
 
-        def load_x(a):
-            rows = x[a * P * PACK : (a + 1) * P * PACK, :].rearrange("(p j) c -> p (j c)", j=PACK)
-            nc.sync.dma_start(raw[a][:].rearrange("p j c -> p (j c)"), rows)
+        def load_x(a, planes, cols, tag):
+            raw = keep.tile([P, planes.stop - planes.start, cols.stop - cols.start], F32, name=tag, tag=tag)
+            nc.sync.dma_start(raw[:], x_rows[a, :, planes, cols])
+            return raw
 
         def load_w(tile, first, last, lo, hi):
             nc.sync.dma_start(tile[:].bitcast(I32), w_words[first:last, :, 2 * lo : 2 * hi].bitcast(I32).rearrange("a p c -> p a c"))
 
-        def load_scales(queue, tile, lo, hi, first=0, end=4):
-            rows = w_scales[:, :, lo:hi].bitcast(I32).rearrange("a (q r) n -> r q a n", r=4)
-            for r in range(first, end):
-                queue.dma_start(tile[r:P:32, :, :].bitcast(I32), rows[r])
+        def load_scales(odd, partition, slot):
+            rows = w_scales.bitcast(I32).rearrange("a (j odd r) n -> odd r (a j) n", odd=2, r=4)
+            nc.sync.dma_start(ws[partition : partition + 4, slot : slot + 2 * PASSES, :].bitcast(I32), rows[odd])
 
-        def load_bias(tile, first, last):
-            with nc.allow_non_contiguous_dma(reason="one bias value a partition and block"):
-                nc.sync.dma_start(tile[:], b.rearrange("(m p) -> p m", p=P)[:, first:last])
+        def move_scales(source, target, count, slot):
+            for a in range(PASSES):
+                nc.vector.tensor_copy(
+                    ws[target : target + count, 2 * a + 1, :].bitcast(I32), ws[source : source + count, 2 * a + slot, :].bitcast(I32)
+                )
 
-        def on_scalar(out, in_):
-            nc.scalar.copy(out, in_)
+        def grouped_tile(tag):
+            return keep.tile([P, HALF, PACK], BF16, name=tag, tag=tag, align_bytes=64)
 
-        def interleave(copy, h, a, lo, hi):
+        def interleave(copy, grouped, raw, planes=slice(0, PACK), lo=0, hi=HALF):
             copy(
-                out=grouped[h][a][:, lo:hi, :].rearrange("p (c i) j -> p c j i", i=4),
-                in_=raw[a][:, :, h * HALF + lo : h * HALF + hi].rearrange("p j (c i) -> p c j i", i=4),
+                out=grouped[:, lo:hi, planes].rearrange("p (c i) j -> p c j i", i=4),
+                in_=raw.rearrange("p j (c i) -> p c j i", i=4),
             )
 
-        def quantize(h, a, lo=0, hi=HALF):
+        def quantize(h, a, grouped, lo=0, hi=HALF):
             nc.vector.quantize_mx(
                 out=codes[h][a][:, lo:hi].bitcast(E4M3X4),
                 scales=scales[h][a][:, lo:hi],
-                in_=grouped[h][a][:, lo:hi, :].rearrange("p c j -> p (c j)"),
+                in_=grouped[:, lo:hi, :].rearrange("p c j -> p (c j)"),
             )
 
         def weights(a, m):
@@ -85,69 +86,84 @@ def tile_list_hscat_bias_kernel(tc, x, w_words, w_scales, b, wgo, offs, out):
 
         def multiply(h, m, bank):
             sums = psum.tile([P, HALF], F32, name=f"sums{h}_{m}", tag=f"bank{bank}")
-            order = list(range(PASSES)) if (h, m) == (0, 0) else [PASSES - 1] + list(range(PASSES - 1))
+            order = ([1, 0, 2], [0, 1, 2])[h] if m == 0 else [2, 0, 1]
             for a in order:
                 nc.tensor.matmul_mx(
                     out=sums[:],
                     lhsT=weights(a, m).bitcast(E2M1X4),
-                    lhsT_scale=(ws_first, ws_rest)[m // 2][:, a, m % 2 * P : (m % 2 + 1) * P],
+                    lhsT_scale=ws[:, 2 * a + 1, m * P : (m + 1) * P],
                     rhs=codes[h][a][:].bitcast(E4M3X4),
                     rhs_scale=scales[h][a][:],
                     start=(a == order[0]),
                     stop=(a == order[-1]),
                 )
-            bias = (b_first, b_rest)[m // 2][:, m % 2 : m % 2 + 1]
+            return sums
+
+        def finish(h, m, sums, bias, tag):
+            biased = keep.tile([P, HALF], F32, name=f"biased{h}_{m}", tag=tag)
             if (h, m) == (0, 0):
-                nc.vector.tensor_scalar(biased[m][:, :HALF], sums[:], bias, None, ADD)
+                nc.vector.tensor_scalar(biased[:], sums[:], bias[:, m : m + 1], None, ADD)
             else:
-                nc.scalar.activation(biased[m][:, h * HALF : (h + 1) * HALF], sums[:], IDENTITY, bias=bias)
+                nc.scalar.activation(biased[:], sums[:], IDENTITY, bias=bias[:, m : m + 1])
+            lists = offs_t[:, h * HALF // 16 : (h + 1) * HALF // 16]
+            nc.vector.tensor_tensor(windows[m][:].indirect(lists), biased[:], wgo_t[h][:], MULT)
 
-        def scatter(m, lo, hi):
-            nc.vector.tensor_tensor(windows[m][:].indirect(offs_t[:, lo // 16 : hi // 16]), biased[m][:, lo:hi], wgo_t[:, lo:hi], MULT)
+        early, late, both = slice(0, HALF), slice(HALF, S), slice(0, S)
+        all_planes, pairs = slice(0, PACK), (slice(0, 2), slice(2, PACK))
 
-        def store(m):
-            pieces = 1 if m >= 2 else 2
-            for lo in range(0, T, T // pieces):
-                nc.sync.dma_start(out[m * P : (m + 1) * P, lo : lo + T // pieces], windows[m][:, lo : lo + T // pieces])
-
-        load_x(0)
-        load_scales(nc.sync, ws_first, 0, M // 2, 0, 2)
-        for a in range(1, PASSES):
-            load_x(a)
-        load_scales(nc.sync, ws_first, 0, M // 2, 2, 4)
+        raw2 = [load_x(2, pairs[0], early, "raw2_0")]
+        nc.vector.memset(ws[96:, 0 : 2 * PASSES : 2, :].bitcast(I32), 0)
+        load_scales(0, 0, 1)
+        nc.sync.dma_start(b_rows[:], b.rearrange("(m p) -> m p", p=P))
+        raw1 = load_x(1, all_planes, early, "raw1")
+        load_scales(1, 96, 0)
+        raw0 = load_x(0, all_planes, both, "raw0")
+        raw2.append(load_x(2, pairs[1], early, "raw2_1"))
         load_w(w_early, 0, PASSES - 1, 0, M // 2)
         load_w(w_last, PASSES - 1, PASSES, 0, M // 2)
-        load_bias(b_first, 0, 2)
+        nc.sync.dma_start(wgo_t[0][:], wgo[:, early])
         nc.sync.dma_start(offs_t[:], offs)
-        nc.sync.dma_start(wgo_t[:], wgo)
         load_w(w_rest, 0, PASSES, M // 2, M)
-        load_bias(b_rest, 2, BLOCKS)
-        load_scales(nc.sync, ws_rest, M // 2, M)
-        for m in range(BLOCKS):
+        raw_late = {a: load_x(a, all_planes, late, f"raw_late{a}") for a in (1, 2)}
+        nc.sync.dma_start(wgo_t[1][:], wgo[:, late])
+
+        nc.vector.memset(b_blocks[:], 0.0)
+        for m in range(BANDS):
             nc.vector.memset(windows[m][:], 0.0)
 
-        for a in range(PASSES - 1):
-            interleave(nc.vector.tensor_copy, 0, a, 0, HALF)
-            interleave(nc.vector.tensor_copy, 1, a, 0, 32)
-            interleave(on_scalar, 1, a, 32, HALF)
-            quantize(0, a)
-            quantize(1, a)
-        a = PASSES - 1
-        interleave(nc.vector.tensor_copy, 0, a, 0, 64)
-        interleave(nc.vector.tensor_copy, 0, a, 64, HALF)
-        interleave(on_scalar, 1, a, 0, HALF)
-        quantize(0, a, 0, 64)
-        quantize(0, a, 64, HALF)
-        quantize(1, a)
+        last = grouped_tile("grouped_last")
+        interleave(nc.scalar.copy, last, raw2[0][:], pairs[0])
+        for q in range(0, P, 32):
+            nc.vector.tensor_copy(b_blocks[q : q + BANDS, :].bitcast(I32), b_rows[:, q : q + 32].bitcast(I32))
+        move_scales(0, 64, 4, 2)
+        b_early = keep.tile([P, 32], F32, name="b_early", tag="grouped_late1", align_bytes=64)
+        nc.vector.transpose(b_early[:], b_blocks[:])
+        nc.vector.transpose(b_late[:], b_blocks[:])
+        move_scales(96, 32, 32, 0)
+        grouped = grouped_tile("grouped_early1")
+        interleave(nc.scalar.copy, grouped, raw1[:])
+        quantize(0, 1, grouped)
+        grouped = grouped_tile("grouped_early0")
+        interleave(nc.vector.tensor_copy, grouped, raw0[:, :, early])
+        for lo in range(0, HALF, PIECE):
+            interleave(nc.vector.tensor_copy, last, raw2[1][:, :, lo : lo + PIECE], pairs[1], lo, lo + PIECE)
+        quantize(0, 0, grouped)
+        for lo in range(0, HALF, PIECE):
+            quantize(0, 2, last, lo, lo + PIECE)
+        grouped = grouped_tile("grouped_late0")
+        interleave(nc.scalar.copy, grouped, raw0[:, :, late])
+        quantize(1, 0, grouped)
 
-        for h in range(2):
-            for m in range(2):
-                multiply(h, m, 2 * m + h)
-                scatter(m, h * HALF, (h + 1) * HALF)
-                if h == 1:
-                    store(m)
-        for m in range(2, BLOCKS):
-            for h in range(2):
-                multiply(h, m, 2 * m + h)
-            scatter(m, 0, S)
-            store(m)
+        for m in range(2):
+            finish(0, m, multiply(0, m, m), b_early, f"biased0_{m}")
+        sums = {m: multiply(0, m, m) for m in (2, 3)}
+        for a in (1, 2):
+            grouped = grouped_tile(f"grouped_late{a}")
+            interleave(nc.scalar.copy, grouped, raw_late[a][:])
+            quantize(1, a, grouped)
+            finish(0, a + 1, sums[a + 1], b_late, f"raw_late{a}")
+        for m in range(BANDS):
+            finish(1, m, multiply(1, m, 1 if m == 0 else 3 + m), b_late, f"biased1_{m}")
+            width = T // (4, 2, 2, 1)[m]
+            for lo in range(0, T, width):
+                nc.sync.dma_start(out[m * P : (m + 1) * P, lo : lo + width], windows[m][:, lo : lo + width])

@@ -31,43 +31,40 @@ def tile_list_hscat_bias_kernel(tc, x, w_words, w_scales, b, wgo, offs, out):
         psum = ctx.enter_context(tc.psum_pool(name="psum", bufs=1))
 
         offs_t = keep.tile([P, S // 16], U16, name="offs_t")
-        w_early = keep.tile([P, PASSES - 1, M], U8, name="w_early", align_bytes=64)
-        w_last = keep.tile([P, 1, M], U8, name="w_last", align_bytes=64)
-        w_rest = keep.tile([P, PASSES, M], U8, name="w_rest", align_bytes=64)
-        ws = keep.tile([P, 2 * PASSES + 1, M], U8, name="ws", align_bytes=64)
-        wgo_t = [keep.tile([P, HALF], F32, name=f"wgo{h}") for h in range(2)]
-        b_rows = keep.tile([BANDS, P], F32, name="b_rows")
-        b_blocks = keep.tile([P, 32], F32, name="b_blocks", align_bytes=64)
-        b_late = keep.tile([P, 32], F32, name="b_late", align_bytes=64)
-        windows = [keep.tile([P, T], F32, name=f"window{m}") for m in range(BANDS)]
-        codes = [[keep.tile([P, HALF], U32, name=f"codes{h}_{a}", align_bytes=64) for a in range(PASSES)] for h in range(2)]
-        scales = [[keep.tile([P, HALF], U8, name=f"scales{h}_{a}", align_bytes=64) for a in range(PASSES)] for h in range(2)]
+        w_early = keep.tile([P, PASSES - 1, M], U8, name="w_early", align_bytes=256)
+        w_last = keep.tile([P, 1, M], U8, name="w_last", align_bytes=256)
+        w_rest = keep.tile([P, PASSES, M], U8, name="w_rest", align_bytes=256)
+        ws = keep.tile([P, PASSES, M], U8, name="ws", align_bytes=256)
+        wgo_t = [keep.tile([P, HALF], F32, name=f"wgo{h}", align_bytes=256) for h in range(2)]
+        b_t = [keep.tile([P, 2], F32, name=f"b{i}") for i in range(2)]
+        windows = [keep.tile([P, T], F32, name=f"window{m}", align_bytes=256) for m in range(BANDS)]
+        codes = [[keep.tile([P, HALF], U32, name=f"codes{h}_{a}", align_bytes=256) for a in range(PASSES)] for h in range(2)]
+        scales = [[keep.tile([P, HALF], U8, name=f"scales{h}_{a}", align_bytes=256) for a in range(PASSES)] for h in range(2)]
         x_rows = x.rearrange("(a p j) c -> a p j c", p=P, j=PACK)
 
-        def load_x(a, planes, cols, tag):
-            raw = keep.tile([P, planes.stop - planes.start, cols.stop - cols.start], F32, name=tag, tag=tag)
-            nc.sync.dma_start(raw[:], x_rows[a, :, planes, cols])
+        def load_x(a, cols, tag):
+            raw = keep.tile([P, PACK, cols.stop - cols.start], F32, name=tag, tag=tag, align_bytes=256)
+            nc.sync.dma_start(raw[:], x_rows[a, :, :, cols])
             return raw
 
         def load_w(tile, first, last, lo, hi):
             nc.sync.dma_start(tile[:].bitcast(I32), w_words[first:last, :, 2 * lo : 2 * hi].bitcast(I32).rearrange("a p c -> p a c"))
 
-        def load_scales(odd, partition, slot):
-            rows = w_scales.bitcast(I32).rearrange("a (j odd r) n -> odd r (a j) n", odd=2, r=4)
-            nc.sync.dma_start(ws[partition : partition + 4, slot : slot + 2 * PASSES, :].bitcast(I32), rows[odd])
+        def load_scales():
+            rows = w_scales.bitcast(I32).rearrange("a (q r) n -> r q a n", r=4)
+            for r in range(4):
+                nc.sync.dma_start(ws[r:P:32, :, :].bitcast(I32), rows[r])
 
-        def move_scales(source, target, count, slot):
-            for a in range(PASSES):
-                nc.vector.tensor_copy(
-                    ws[target : target + count, 2 * a + 1, :].bitcast(I32), ws[source : source + count, 2 * a + slot, :].bitcast(I32)
-                )
+        def load_bias(i):
+            with nc.allow_non_contiguous_dma(reason="one bias value a partition and band"):
+                nc.sync.dma_start(b_t[i][:], b.rearrange("(m p) -> p m", p=P)[:, 2 * i : 2 * i + 2])
 
         def grouped_tile(tag):
-            return keep.tile([P, HALF, PACK], BF16, name=tag, tag=tag, align_bytes=64)
+            return keep.tile([P, HALF, PACK], BF16, name=tag, tag=tag, align_bytes=256)
 
-        def interleave(copy, grouped, raw, planes=slice(0, PACK), lo=0, hi=HALF):
+        def interleave(copy, grouped, raw, lo=0, hi=HALF):
             copy(
-                out=grouped[:, lo:hi, planes].rearrange("p (c i) j -> p c j i", i=4),
+                out=grouped[:, lo:hi, :].rearrange("p (c i) j -> p c j i", i=4),
                 in_=raw.rearrange("p j (c i) -> p c j i", i=4),
             )
 
@@ -86,12 +83,12 @@ def tile_list_hscat_bias_kernel(tc, x, w_words, w_scales, b, wgo, offs, out):
 
         def multiply(h, m, bank):
             sums = psum.tile([P, HALF], F32, name=f"sums{h}_{m}", tag=f"bank{bank}")
-            order = ([1, 0, 2], [0, 1, 2])[h] if m == 0 else [2, 0, 1]
+            order = [0, 1, 2] if m == 0 else [2, 0, 1]
             for a in order:
                 nc.tensor.matmul_mx(
                     out=sums[:],
                     lhsT=weights(a, m).bitcast(E2M1X4),
-                    lhsT_scale=ws[:, 2 * a + 1, m * P : (m + 1) * P],
+                    lhsT_scale=ws[:, a, m * P : (m + 1) * P],
                     rhs=codes[h][a][:].bitcast(E4M3X4),
                     rhs_scale=scales[h][a][:],
                     start=(a == order[0]),
@@ -99,71 +96,55 @@ def tile_list_hscat_bias_kernel(tc, x, w_words, w_scales, b, wgo, offs, out):
                 )
             return sums
 
-        def finish(h, m, sums, bias, tag):
-            biased = keep.tile([P, HALF], F32, name=f"biased{h}_{m}", tag=tag)
+        def finish(h, m, sums, tag):
+            bias = b_t[m // 2][:, m % 2 : m % 2 + 1]
+            biased = keep.tile([P, HALF], F32, name=f"biased{h}_{m}", tag=tag, align_bytes=256)
             if (h, m) == (0, 0):
-                nc.vector.tensor_scalar(biased[:], sums[:], bias[:, m : m + 1], None, ADD)
+                nc.vector.tensor_scalar(biased[:], sums[:], bias, None, ADD)
             else:
-                nc.scalar.activation(biased[:], sums[:], IDENTITY, bias=bias[:, m : m + 1])
+                nc.scalar.activation(biased[:], sums[:], IDENTITY, bias=bias)
             lists = offs_t[:, h * HALF // 16 : (h + 1) * HALF // 16]
             nc.vector.tensor_tensor(windows[m][:].indirect(lists), biased[:], wgo_t[h][:], MULT)
 
-        early, late, both = slice(0, HALF), slice(HALF, S), slice(0, S)
-        all_planes, pairs = slice(0, PACK), (slice(0, 2), slice(2, PACK))
+        early, late = slice(0, HALF), slice(HALF, S)
 
-        raw2 = [load_x(2, pairs[0], early, "raw2_0")]
-        nc.vector.memset(ws[96:, 0 : 2 * PASSES : 2, :].bitcast(I32), 0)
-        load_scales(0, 0, 1)
-        nc.sync.dma_start(b_rows[:], b.rearrange("(m p) -> m p", p=P))
-        raw1 = load_x(1, all_planes, early, "raw1")
-        load_scales(1, 96, 0)
-        raw0 = load_x(0, all_planes, both, "raw0")
-        raw2.append(load_x(2, pairs[1], early, "raw2_1"))
+        raw = [load_x(0, early, "raw0")]
+        load_scales()
+        raw += [load_x(a, early, f"raw{a}") for a in (1, 2)]
         load_w(w_early, 0, PASSES - 1, 0, M // 2)
         load_w(w_last, PASSES - 1, PASSES, 0, M // 2)
-        nc.sync.dma_start(wgo_t[0][:], wgo[:, early])
+        load_bias(0)
         nc.sync.dma_start(offs_t[:], offs)
+        nc.sync.dma_start(wgo_t[0][:], wgo[:, early])
         load_w(w_rest, 0, PASSES, M // 2, M)
-        raw_late = {a: load_x(a, all_planes, late, f"raw_late{a}") for a in (1, 2)}
+        raw_late = [load_x(0, late, "raw_late0")]
+        load_bias(1)
+        raw_late += [load_x(a, late, f"raw_late{a}") for a in (1, 2)]
         nc.sync.dma_start(wgo_t[1][:], wgo[:, late])
-
-        nc.vector.memset(b_blocks[:], 0.0)
         for m in range(BANDS):
             nc.vector.memset(windows[m][:], 0.0)
 
-        last = grouped_tile("grouped_last")
-        interleave(nc.scalar.copy, last, raw2[0][:], pairs[0])
-        for q in range(0, P, 32):
-            nc.vector.tensor_copy(b_blocks[q : q + BANDS, :].bitcast(I32), b_rows[:, q : q + 32].bitcast(I32))
-        move_scales(0, 64, 4, 2)
-        b_early = keep.tile([P, 32], F32, name="b_early", tag="grouped_late1", align_bytes=64)
-        nc.vector.transpose(b_early[:], b_blocks[:])
-        nc.vector.transpose(b_late[:], b_blocks[:])
-        move_scales(96, 32, 32, 0)
-        grouped = grouped_tile("grouped_early1")
-        interleave(nc.scalar.copy, grouped, raw1[:])
-        quantize(0, 1, grouped)
-        grouped = grouped_tile("grouped_early0")
-        interleave(nc.vector.tensor_copy, grouped, raw0[:, :, early])
+        grouped = [grouped_tile(f"grouped_early{a}") for a in range(PASSES)]
+        for a in range(PASSES - 1):
+            interleave(nc.vector.tensor_copy, grouped[a], raw[a][:, :, :PIECE], 0, PIECE)
+            interleave(nc.scalar.copy, grouped[a], raw[a][:, :, PIECE:], PIECE, HALF)
+            quantize(0, a, grouped[a])
         for lo in range(0, HALF, PIECE):
-            interleave(nc.vector.tensor_copy, last, raw2[1][:, :, lo : lo + PIECE], pairs[1], lo, lo + PIECE)
-        quantize(0, 0, grouped)
+            interleave(nc.vector.tensor_copy, grouped[2], raw[2][:, :, lo : lo + PIECE], lo, lo + PIECE)
         for lo in range(0, HALF, PIECE):
-            quantize(0, 2, last, lo, lo + PIECE)
-        grouped = grouped_tile("grouped_late0")
-        interleave(nc.scalar.copy, grouped, raw0[:, :, late])
-        quantize(1, 0, grouped)
+            quantize(0, 2, grouped[2], lo, lo + PIECE)
 
         for m in range(2):
-            finish(0, m, multiply(0, m, m), b_early, f"biased0_{m}")
+            finish(0, m, multiply(0, m, m), f"biased0_{m}")
         sums = {m: multiply(0, m, m) for m in (2, 3)}
-        for a in (1, 2):
+        for a in range(PASSES):
             grouped = grouped_tile(f"grouped_late{a}")
             interleave(nc.scalar.copy, grouped, raw_late[a][:])
             quantize(1, a, grouped)
-            finish(0, a + 1, sums[a + 1], b_late, f"raw_late{a}")
+            if a != 1:
+                finish(0, 2 + a // 2, sums[2 + a // 2], f"raw_late{a}")
         for m in range(BANDS):
-            finish(1, m, multiply(1, m, 1 if m == 0 else 3 + m), b_late, f"biased1_{m}")
-            width = T // (4, 2, 2, 1)[m]
+            finish(1, m, multiply(1, m, 1 if m == 0 else 3 + m), f"biased1_{m}")
+            width = T // 2 if m < 2 else T
             for lo in range(0, T, width):
                 nc.sync.dma_start(out[m * P : (m + 1) * P, lo : lo + width], windows[m][:, lo : lo + width])

@@ -125,12 +125,11 @@ def tile_list_hscat_bias_kernel(tc, x, w_words, w_scales, b, wgo, offs, out):
             nc.vector.memset(windows[m][:], 0.0)
 
         grouped = [grouped_tile(f"grouped_early{a}") for a in range(PASSES)]
-        for a in range(PASSES - 1):
+        for a in range(PASSES):
             interleave(nc.vector.tensor_copy, grouped[a], raw[a][:, :, :PIECE], 0, PIECE)
             interleave(nc.scalar.copy, grouped[a], raw[a][:, :, PIECE:], PIECE, HALF)
-            quantize(0, a, grouped[a])
-        for lo in range(0, HALF, PIECE):
-            interleave(nc.vector.tensor_copy, grouped[2], raw[2][:, :, lo : lo + PIECE], lo, lo + PIECE)
+            if a < PASSES - 1:
+                quantize(0, a, grouped[a])
         for lo in range(0, HALF, PIECE):
             quantize(0, 2, grouped[2], lo, lo + PIECE)
 

@@ -126,11 +126,12 @@ def tile_list_hscat_bias_kernel(tc, x, w_words, w_scales, b, wgo, offs, out):
 
         grouped = [grouped_tile(f"grouped_early{a}") for a in range(PASSES)]
         for a in range(PASSES):
-            interleave(nc.vector.tensor_copy, grouped[a], raw[a][:, :, :PIECE], 0, PIECE)
-            interleave(nc.scalar.copy, grouped[a], raw[a][:, :, PIECE:], PIECE, HALF)
+            share = PIECE if a < PASSES - 1 else PIECE - 8
+            interleave(nc.vector.tensor_copy, grouped[a], raw[a][:, :, :share], 0, share)
+            interleave(nc.scalar.copy, grouped[a], raw[a][:, :, share:], share, HALF)
             if a < PASSES - 1:
                 quantize(0, a, grouped[a])
-        for lo in range(0, HALF, PIECE):
+        for lo in (PIECE, 0):
             quantize(0, 2, grouped[2], lo, lo + PIECE)
 
         for m in range(2):

@@ -33,10 +33,10 @@ def tile_list_hscat_bias_kernel(tc, x, w_words, w_scales, b, wgo, offs, out):
         offs_t = keep.tile([P, S // 16], U16, name="offs_t")
         w_early = keep.tile([P, PASSES - 1, M], U8, name="w_early", align_bytes=256)
         w_last = keep.tile([P, 1, M], U8, name="w_last", align_bytes=256)
-        w_rest = keep.tile([P, PASSES, M], U8, name="w_rest", align_bytes=256)
+        w_rest = [keep.tile([P, PASSES, 2 * P], U8, name=f"w_rest{i}", align_bytes=256) for i in range(2)]
         ws = keep.tile([P, PASSES, M], U8, name="ws", align_bytes=256)
         wgo_t = [keep.tile([P, HALF], F32, name=f"wgo{h}", align_bytes=256) for h in range(2)]
-        b_t = [keep.tile([P, 2], F32, name=f"b{i}") for i in range(2)]
+        b_t = keep.tile([P, BANDS], F32, name="b_t")
         windows = [keep.tile([P, T], F32, name=f"window{m}", align_bytes=256) for m in range(BANDS)]
         codes = [[keep.tile([P, HALF], U32, name=f"codes{h}_{a}", align_bytes=256) for a in range(PASSES)] for h in range(2)]
         scales = [[keep.tile([P, HALF], U8, name=f"scales{h}_{a}", align_bytes=256) for a in range(PASSES)] for h in range(2)]
@@ -55,9 +55,9 @@ def tile_list_hscat_bias_kernel(tc, x, w_words, w_scales, b, wgo, offs, out):
             for r in range(4):
                 nc.sync.dma_start(ws[r:P:32, :, :].bitcast(I32), rows[r])
 
-        def load_bias(i):
+        def load_bias(tile, first, last):
             with nc.allow_non_contiguous_dma(reason="one bias value a partition and band"):
-                nc.sync.dma_start(b_t[i][:], b.rearrange("(m p) -> p m", p=P)[:, 2 * i : 2 * i + 2])
+                nc.sync.dma_start(tile[:], b.rearrange("(m p) -> p m", p=P)[:, first:last])
 
         def grouped_tile(tag):
             return keep.tile([P, HALF, PACK], BF16, name=tag, tag=tag, align_bytes=256)
@@ -78,7 +78,7 @@ def tile_list_hscat_bias_kernel(tc, x, w_words, w_scales, b, wgo, offs, out):
         def weights(a, m):
             cols = slice(m % 2 * 2 * P, (m % 2 + 1) * 2 * P)
             if m >= 2:
-                return w_rest[:, a, cols]
+                return w_rest[m - 2][:, a, :]
             return w_early[:, a, cols] if a < PASSES - 1 else w_last[:, 0, cols]
 
         def multiply(h, m, bank):
@@ -97,7 +97,7 @@ def tile_list_hscat_bias_kernel(tc, x, w_words, w_scales, b, wgo, offs, out):
             return sums
 
         def finish(h, m, sums, tag):
-            bias = b_t[m // 2][:, m % 2 : m % 2 + 1]
+            bias = b_t[:, m : m + 1]
             biased = keep.tile([P, HALF], F32, name=f"biased{h}_{m}", tag=tag, align_bytes=256)
             if (h, m) == (0, 0):
                 nc.vector.tensor_scalar(biased[:], sums[:], bias, None, ADD)
@@ -113,13 +113,13 @@ def tile_list_hscat_bias_kernel(tc, x, w_words, w_scales, b, wgo, offs, out):
         raw += [load_x(a, early, f"raw{a}") for a in (1, 2)]
         load_w(w_early, 0, PASSES - 1, 0, M // 2)
         load_w(w_last, PASSES - 1, PASSES, 0, M // 2)
-        load_bias(0)
+        load_bias(b_t, 0, BANDS)
         nc.sync.dma_start(offs_t[:], offs)
         nc.sync.dma_start(wgo_t[0][:], wgo[:, early])
-        load_w(w_rest, 0, PASSES, M // 2, M)
         raw_late = [load_x(0, late, "raw_late0")]
-        load_bias(1)
+        load_w(w_rest[0], 0, PASSES, 2 * P, 3 * P)
         raw_late += [load_x(a, late, f"raw_late{a}") for a in (1, 2)]
+        load_w(w_rest[1], 0, PASSES, 3 * P, M)
         nc.sync.dma_start(wgo_t[1][:], wgo[:, late])
         for m in range(BANDS):
             nc.vector.memset(windows[m][:], 0.0)
@@ -139,12 +139,15 @@ def tile_list_hscat_bias_kernel(tc, x, w_words, w_scales, b, wgo, offs, out):
         sums = {m: multiply(0, m, m) for m in (2, 3)}
         for a in range(PASSES):
             grouped = grouped_tile(f"grouped_late{a}")
-            interleave(nc.scalar.copy, grouped, raw_late[a][:])
+            share = PIECE if a == PASSES - 1 else 0
+            if share:
+                interleave(nc.vector.tensor_copy, grouped, raw_late[a][:, :, :share], 0, share)
+            interleave(nc.scalar.copy, grouped, raw_late[a][:, :, share:], share, HALF)
             quantize(1, a, grouped)
-            if a != 1:
-                finish(0, 2 + a // 2, sums[2 + a // 2], f"raw_late{a}")
+        finish(0, 2, sums[2], "raw_late1")
+        finish(0, 3, sums[3], "biased0_3")
         for m in range(BANDS):
-            finish(1, m, multiply(1, m, 1 if m == 0 else 3 + m), f"biased1_{m}")
+            finish(1, m, multiply(1, m, 2 + m % 2), f"biased1_{m}")
             width = T // 2 if m < 2 else T
             for lo in range(0, T, width):
                 nc.sync.dma_start(out[m * P : (m + 1) * P, lo : lo + width], windows[m][:, lo : lo + width])

from contextlib import ExitStack

import concourse.mybir as mybir

F32 = mybir.dt.float32
BF16 = mybir.dt.bfloat16
I32 = mybir.dt.int32
U32 = mybir.dt.uint32
U16 = mybir.dt.uint16
U8 = mybir.dt.uint8
E4M3X4 = mybir.dt.float8_e4m3fn_x4
E2M1X4 = mybir.dt.float4_e2m1fn_x4
IDENTITY = mybir.ActivationFunctionType.Identity
MULT = mybir.AluOpType.mult
ADD = mybir.AluOpType.add

K, M, T, S = 1536, 512, 512, 256
P = 128
PACK = 4
PASSES = K // (P * PACK)
BANDS = M // P
HALF = S // 2
PIECE = HALF // 2
FLOPS = 2 * K * M * S


def tile_list_hscat_bias_kernel(tc, x, w_words, w_scales, b, wgo, offs, out):
    nc = tc.nc
    with ExitStack() as ctx:
        keep = ctx.enter_context(tc.tile_pool(name="keep", bufs=1))
        psum = ctx.enter_context(tc.psum_pool(name="psum", bufs=1))

        offs_t = keep.tile([P, S // 16], U16, name="offs_t")
        w_early = keep.tile([P, PASSES - 1, M], U8, name="w_early", align_bytes=256)
        w_last = keep.tile([P, 1, M], U8, name="w_last", align_bytes=256)
        w_rest = [keep.tile([P, PASSES, 2 * P], U8, name=f"w_rest{i}", align_bytes=256) for i in range(2)]
        ws = keep.tile([P, PASSES, M], U8, name="ws", align_bytes=256)
        wgo_t = [keep.tile([P, HALF], F32, name=f"wgo{h}", align_bytes=256) for h in range(2)]
        b_t = keep.tile([P, BANDS], F32, name="b_t")
        windows = [keep.tile([P, T], F32, name=f"window{m}", align_bytes=256) for m in range(BANDS)]
        codes = [[keep.tile([P, HALF], U32, name=f"codes{h}_{a}", align_bytes=256) for a in range(PASSES)] for h in range(2)]
        scales = [[keep.tile([P, HALF], U8, name=f"scales{h}_{a}", align_bytes=256) for a in range(PASSES)] for h in range(2)]
        x_rows = x.rearrange("(a p j) c -> a p j c", p=P, j=PACK)

        def load_x(a, cols, tag):
            raw = keep.tile([P, PACK, cols.stop - cols.start], F32, name=tag, tag=tag, align_bytes=256)
            nc.sync.dma_start(raw[:], x_rows[a, :, :, cols])
            return raw

        def load_w(tile, first, last, lo, hi):
            nc.sync.dma_start(tile[:].bitcast(I32), w_words[first:last, :, 2 * lo : 2 * hi].bitcast(I32).rearrange("a p c -> p a c"))

        def load_scales():
            rows = w_scales.bitcast(I32).rearrange("a (q r) n -> r q a n", r=4)
            for r in range(4):
                nc.sync.dma_start(ws[r:P:32, :, :].bitcast(I32), rows[r])

        def load_bias(tile, first, last):
            with nc.allow_non_contiguous_dma(reason="one bias value a partition and band"):
                nc.sync.dma_start(tile[:], b.rearrange("(m p) -> p m", p=P)[:, first:last])

        def grouped_tile(tag):
            return keep.tile([P, HALF, PACK], BF16, name=tag, tag=tag, align_bytes=256)

        def interleave(copy, grouped, raw, lo=0, hi=HALF):
            copy(
                out=grouped[:, lo:hi, :].rearrange("p (c i) j -> p c j i", i=4),
                in_=raw.rearrange("p j (c i) -> p c j i", i=4),
            )

        def quantize(h, a, grouped, lo=0, hi=HALF):
            nc.vector.quantize_mx(
                out=codes[h][a][:, lo:hi].bitcast(E4M3X4),
                scales=scales[h][a][:, lo:hi],
                in_=grouped[:, lo:hi, :].rearrange("p c j -> p (c j)"),
            )

        def weights(a, m):
            cols = slice(m % 2 * 2 * P, (m % 2 + 1) * 2 * P)
            if m >= 2:
                return w_rest[m - 2][:, a, :]
            return w_early[:, a, cols] if a < PASSES - 1 else w_last[:, 0, cols]

        def multiply(h, m, bank):
            sums = psum.tile([P, HALF], F32, name=f"sums{h}_{m}", tag=f"bank{bank}")
            order = [0, 1, 2] if m == 0 else [2, 0, 1]
            for a in order:
                nc.tensor.matmul_mx(
                    out=sums[:],
                    lhsT=weights(a, m).bitcast(E2M1X4),
                    lhsT_scale=ws[:, a, m * P : (m + 1) * P],
                    rhs=codes[h][a][:].bitcast(E4M3X4),
                    rhs_scale=scales[h][a][:],
                    start=(a == order[0]),
                    stop=(a == order[-1]),
                )
            return sums

        def finish(h, m, sums, tag):
            bias = b_t[:, m : m + 1]
            biased = keep.tile([P, HALF], F32, name=f"biased{h}_{m}", tag=tag, align_bytes=256)
            if (h, m) == (0, 0):
                nc.vector.tensor_scalar(biased[:], sums[:], bias, None, ADD)
            else:
                nc.scalar.activation(biased[:], sums[:], IDENTITY, bias=bias)
            lists = offs_t[:, h * HALF // 16 : (h + 1) * HALF // 16]
            nc.vector.tensor_tensor(windows[m][:].indirect(lists), biased[:], wgo_t[h][:], MULT)

        early, late = slice(0, HALF), slice(HALF, S)

        raw = [load_x(0, early, "raw0")]
        load_scales()
        raw += [load_x(a, early, f"raw{a}") for a in (1, 2)]
        load_w(w_early, 0, PASSES - 1, 0, M // 2)
        load_w(w_last, PASSES - 1, PASSES, 0, M // 2)
        load_bias(b_t, 0, BANDS)
        nc.sync.dma_start(offs_t[:], offs)
        nc.sync.dma_start(wgo_t[0][:], wgo[:, early])
        raw_late = [load_x(0, late, "raw_late0")]
        load_w(w_rest[0], 0, PASSES, 2 * P, 3 * P)
        raw_late += [load_x(a, late, f"raw_late{a}") for a in (1, 2)]
        load_w(w_rest[1], 0, PASSES, 3 * P, M)
        nc.sync.dma_start(wgo_t[1][:], wgo[:, late])
        for m in range(BANDS):
            nc.vector.memset(windows[m][:], 0.0)

        grouped = [grouped_tile(f"grouped_early{a}") for a in range(PASSES)]
        for a in range(PASSES):
            share = PIECE if a < PASSES - 1 else PIECE - 8
            interleave(nc.vector.tensor_copy, grouped[a], raw[a][:, :, :share], 0, share)
            interleave(nc.scalar.copy, grouped[a], raw[a][:, :, share:], share, HALF)
            if a < PASSES - 1:
                quantize(0, a, grouped[a])
        for lo in (PIECE, 0):
            quantize(0, 2, grouped[2], lo, lo + PIECE)

        for m in range(2):
            finish(0, m, multiply(0, m, m), f"biased0_{m}")
        sums = {m: multiply(0, m, m) for m in (2, 3)}
        for a in range(PASSES):
            grouped = grouped_tile(f"grouped_late{a}")
            share = PIECE if a == PASSES - 1 else 0
            if share:
                interleave(nc.vector.tensor_copy, grouped, raw_late[a][:, :, :share], 0, share)
            interleave(nc.scalar.copy, grouped, raw_late[a][:, :, share:], share, HALF)
            quantize(1, a, grouped)
        finish(0, 2, sums[2], "raw_late1")
        finish(0, 3, sums[3], "biased0_3")
        for m in range(BANDS):
            finish(1, m, multiply(1, m, 2 + m % 2), f"biased1_{m}")
            width = T // 2 if m < 2 else T
            for lo in range(0, T, width):
                nc.sync.dma_start(out[m * P : (m + 1) * P, lo : lo + width], windows[m][:, lo : lo + width])
